import numpy as np
import ml_dtypes


def mxq(x, axis, fmt="e4m3"):
    dtype, down = {"e4m3": (ml_dtypes.float8_e4m3fn, 7), "e5m2": (ml_dtypes.float8_e5m2, 14)}[fmt]
    v = np.moveaxis(np.asarray(x, np.float32).astype(ml_dtypes.bfloat16).astype(np.float64), axis, -1)
    blocks = v.reshape(v.shape[:-1] + (-1, 32))
    amax = np.abs(blocks).max(-1, keepdims=True)
    byte = np.maximum(np.where(amax > 0, np.frexp(amax)[1] - 1 + 127, 0) - down, 1)
    scale = np.exp2(byte - 127.0)
    codes = (blocks / scale).astype(np.float32).astype(dtype).astype(np.float64)
    return np.moveaxis((codes * scale).reshape(v.shape), -1, axis)


WIDE = False


def mx_kscale(k):
    if not WIDE:
        return np.ones(k)
    levels = np.array([10, -10, 5, -5, 0])
    if k % 512:
        return np.exp2(np.random.permutation(np.resize(levels, k // 32))).repeat(32)
    a = np.empty((k // 512, 16))
    for p in range(k // 512):
        a[p, :8] = np.random.permutation(np.resize(levels, 8))
        for g in range(8):
            far = levels[np.abs(levels - a[p, g]) >= 10]
            a[p, g + 8] = far[np.random.randint(len(far))]
    return np.exp2(a.ravel()).repeat(32)


BF16 = ml_dtypes.bfloat16


def bf(x):
    return np.asarray(x, np.float32).astype(BF16)


def f64(x):
    return np.asarray(x).astype(np.float64)


B, D, R, E = 128, 3072, 2048, 2


def softmax(g):
    e = np.exp(g - g.max(axis=-1, keepdims=True))
    return e / e.sum(axis=-1, keepdims=True)


def draw0():
    s, t = mx_kscale(D), mx_kscale(R)
    x0 = bf(np.random.standard_normal((B, D)) * s)
    x = bf(np.random.standard_normal((B, D)) * s)
    v = bf(np.random.standard_normal((E, D, R)) / np.sqrt(D) / s[None, :, None])
    c = bf((1.0 + 0.1 * np.random.standard_normal((E, R))) * t)
    u = bf(1.5 * np.random.standard_normal((E, R, D)) / np.sqrt(R) / t[None, :, None])
    bias = bf(0.3 * np.random.standard_normal(D))
    gate_logits = bf(np.random.standard_normal((B, E)))
    return {"x0": x0, "x": x, "v": v, "c": c, "u": u, "bias": bias, "gate_logits": gate_logits}


def expert_outputs(x, v, c, u):
    a = mxq(x, 1, "e4m3") @ mxq(v, 1, "e4m3")
    h = np.tanh(a) * c[:, None, :]
    return mxq(h, 2, "e4m3") @ mxq(u, 1, "e4m3")


def core(x0, x, v, c, u, bias, gate_logits):
    y = expert_outputs(f64(x), f64(v), f64(c), f64(u))
    p = softmax(f64(gate_logits))
    weights = np.transpose(p)[:, :, None]
    m = np.sum(weights * y, axis=0)
    return f64(x0) * (m + f64(bias)[None, :]) + f64(x)


def e4m3fn_bytes(y):
    return np.clip(np.asarray(y, np.float64), -448.0, 448.0).astype(np.float32).astype(ml_dtypes.float8_e4m3fn).view(np.uint8)


def e4m3fn_values(b):
    return np.asarray(b, np.uint8).view(ml_dtypes.float8_e4m3fn).astype(np.float64)


def setup_inputs():
    d = draw0()
    x0 = np.asarray(d['v']).astype(np.float64)
    s = (np.max(np.abs(x0), axis=(0, 2), keepdims=True) / 448.0).astype(np.float32)
    out = {}
    for k, v in d.items():
        if k == 'v':
            out['v_bytes'] = e4m3fn_bytes(x0 / s.astype(np.float64))
            out['v_scale'] = s
        else:
            out[k] = v
    return out


def reference(x0, x, v_bytes, v_scale, c, u, bias, gate_logits):
    return core(x0, x, e4m3fn_values(v_bytes) * v_scale.astype(np.float64), c, u, bias, gate_logits)

@@ -1,0 +1,285 @@
+from contextlib import ExitStack
+
+import concourse.mybir as mybir
+from concourse.masks import make_identity
+
+B, D, R, E = 128, 3072, 2048, 2
+P = 128
+PACK = 4
+K_PASS = P * PACK
+FLOPS = 2 * 2 * E * B * D * R
+
+F32 = mybir.dt.float32
+BF16 = mybir.dt.bfloat16
+U32 = mybir.dt.uint32
+U8 = mybir.dt.uint8
+FP8 = mybir.dt.float8_e4m3fn
+FP8X4 = mybir.dt.float8_e4m3fn_x4
+ACT = mybir.ActivationFunctionType
+ALU = mybir.AluOpType
+AX = mybir.AxisListType
+
+W = 1024
+NB = 512
+V_PASSES = D // K_PASS
+U_PASSES = R // K_PASS
+RH = R // W
+DB = D // W
+V_WIDEN = 352
+U_VEC = 448
+
+
+def tile_dcnv2lowrankexpertcross_w_kernel(tc, x0, x, v_bytes, v_scale, c, u, bias, gate_logits, out):
+    nc = tc.nc
+    with ExitStack() as ctx:
+        const = ctx.enter_context(tc.tile_pool(name="const", bufs=1))
+        byte_pool = ctx.enter_context(tc.tile_pool(name="byte_pool", bufs=6))
+        wide_pool = ctx.enter_context(tc.tile_pool(name="wide_pool", bufs=3))
+        raw_pool = ctx.enter_context(tc.tile_pool(name="raw_pool", bufs=8))
+        inter_pool = ctx.enter_context(tc.tile_pool(name="inter_pool", bufs=3))
+        code_pool = ctx.enter_context(tc.tile_pool(name="code_pool", bufs=4))
+        small = ctx.enter_context(tc.tile_pool(name="small", bufs=2))
+        mix = ctx.enter_context(tc.tile_pool(name="mix", bufs=2))
+        acc_pool = ctx.enter_context(tc.psum_pool(name="acc_pool", bufs=4))
+        tr_pool = ctx.enter_context(tc.psum_pool(name="tr_pool", bufs=4))
+
+        ident = const.tile([P, P], F32)
+        scale_sb = const.tile([P, V_PASSES, PACK], F32)
+        x_sb = const.tile([B, D], BF16)
+        x0_sb = const.tile([B, D], BF16)
+        bias_sb = const.tile([B, D], BF16)
+        c_sb = const.tile([B, E, R], BF16)
+        gate_sb = const.tile([B, E], BF16)
+        x_codes = const.tile([P, V_PASSES, B], U32, align_bytes=64)
+        x_scales = const.tile([P, V_PASSES, B], U8, align_bytes=64)
+        h_codes = const.tile([P, E, U_PASSES, B], U32, align_bytes=64)
+        h_scales = const.tile([P, E, U_PASSES, B], U8, align_bytes=64)
+
+        units = [("v", e, hb, g) for e in range(E) for hb in range(RH) for g in range(V_PASSES)]
+        n_v = len(units)
+        units += [("u", e, db, g) for db in range(DB) for e in range(E) for g in range(U_PASSES)]
+        n = len(units)
+        raw = {}
+        wide = {}
+        inter = {}
+        codes = {}
+        accs = {}
+        hid = {}
+        mixed = {}
+        gates = {}
+
+        def load(i):
+            kind, e, blk, g = units[i]
+            ks = slice(g * K_PASS, (g + 1) * K_PASS)
+            cs = slice(blk * W, (blk + 1) * W)
+            if kind == "v":
+                v_raw = byte_pool.tile([P, PACK, W], U8)
+                nc.sync.dma_start(out=v_raw[:], in_=v_bytes[e, ks, cs].rearrange("(p t) w -> p t w", t=PACK))
+                raw[i] = v_raw
+            else:
+                u_raw = raw_pool.tile([P, PACK, W], BF16)
+                nc.sync.dma_start(out=u_raw[:], in_=u[e, ks, cs].rearrange("(p t) w -> p t w", t=PACK))
+                raw[i] = u_raw
+
+        def widen(i):
+            kind, e, blk, g = units[i]
+            if kind == "u":
+                return
+            v_wide = wide_pool.tile([P, PACK, W], BF16)
+            v_raw = raw.pop(i)
+            cut = W - V_WIDEN
+            nc.vector.tensor_scalar(
+                out=v_wide[:, 3, cut:], in0=v_raw[:, 3, cut:].bitcast(FP8),
+                scalar1=scale_sb[:, g, 3:4], scalar2=None, op0=ALU.mult)
+            for t in range(PACK):
+                end = W if t < 3 else cut
+                nc.scalar.activation(
+                    out=v_wide[:, t, :end], in_=v_raw[:, t, :end].bitcast(FP8),
+                    func=ACT.Copy, scale=scale_sb[:, g, t:t + 1])
+            wide[i] = v_wide
+
+        def interleave(copy, dst, src):
+            copy(out=dst.rearrange("p (c i) t -> p c t i", i=4), in_=src.rearrange("p t (c i) -> p c t i", i=4))
+
+        def arrange(i):
+            kind, e, blk, g = units[i]
+            grouped = inter_pool.tile([P, W, PACK], BF16, align_bytes=64)
+            if kind == "v":
+                interleave(nc.vector.tensor_copy, grouped[:], wide.pop(i)[:])
+            else:
+                u_raw = raw.pop(i)
+                interleave(nc.vector.tensor_copy, grouped[:, :U_VEC, :], u_raw[:, :, :U_VEC])
+                interleave(nc.scalar.copy, grouped[:, U_VEC:, :], u_raw[:, :, U_VEC:])
+            inter[i] = grouped
+
+        def quantize(i):
+            w_codes = code_pool.tile([P, W], U32, align_bytes=64)
+            w_scales = code_pool.tile([P, W], U8, align_bytes=64)
+            nc.vector.quantize_mx(
+                out=w_codes[:].bitcast(FP8X4), scales=w_scales[:],
+                in_=inter.pop(i)[:].rearrange("p w t -> p (w t)"))
+            codes[i] = (w_codes, w_scales)
+
+        def multiply(i):
+            kind, e, blk, g = units[i]
+            w_codes, w_scales = codes.pop(i)
+            last = (V_PASSES if kind == "v" else U_PASSES) - 1
+            if g == 0:
+                banks = []
+                for j in range(W // NB):
+                    acc = acc_pool.tile([B, NB], F32)
+                    banks.append(acc)
+                accs[(kind, e, blk)] = banks
+            banks = accs[(kind, e, blk)]
+            for j in range(W // NB):
+                js = slice(j * NB, (j + 1) * NB)
+                lhs = x_codes[:, g, :] if kind == "v" else h_codes[:, e, g, :]
+                lhs_scale = x_scales[:, g, :] if kind == "v" else h_scales[:, e, g, :]
+                nc.tensor.matmul_mx(
+                    out=banks[j][:], lhsT=lhs.bitcast(FP8X4), lhsT_scale=lhs_scale,
+                    rhs=w_codes[:, js].bitcast(FP8X4), rhs_scale=w_scales[:, js],
+                    start=(g == 0), stop=(g == last))
+
+        def turn(src_words, q, slots):
+            for j in range(2):
+                for w in range(2):
+                    first = 256 * (2 * q + j)
+                    nc.tensor.transpose(slots[:, 2 * j + w, :], src_words[:, first + w:first + 256:2], ident[:])
+
+        def group_words(dst, slots):
+            nc.vector.tensor_copy(
+                out=dst.bitcast(F32).rearrange("p (j r w) -> p j r w", j=2, w=2),
+                in_=slots.rearrange("p (j w) r -> p j r w", w=2))
+
+        def hidden_tanh(e, hb):
+            th = small.tile([B, W], F32)
+            for j, acc in enumerate(accs.pop(("v", e, hb))):
+                nc.scalar.activation(out=th[:, j * NB:(j + 1) * NB], in_=acc[:], func=ACT.Tanh)
+            hid[(e, hb)] = th
+
+        def hidden_scale(e, hb):
+            h = small.tile([B, W], BF16)
+            nc.vector.tensor_tensor(out=h[:], in0=hid[(e, hb)][:], in1=c_sb[:, e, hb * W:(hb + 1) * W], op=ALU.mult)
+            slots = tr_pool.tile([P, 4, B], F32)
+            turn(h[:].bitcast(F32), 0, slots)
+            hid[(e, hb)] = slots
+
+        def hidden_group(e, hb):
+            hg = small.tile([P, 2 * B * PACK], BF16, align_bytes=64)
+            group_words(hg[:], hid[(e, hb)][:])
+            hid[(e, hb)] = hg
+
+        def hidden_quantize(e, hb):
+            gs = slice(2 * hb, 2 * hb + 2)
+            nc.vector.quantize_mx(
+                out=h_codes[:, e, gs, :].rearrange("p g b -> p (g b)").bitcast(FP8X4),
+                scales=h_scales[:, e, gs, :].rearrange("p g b -> p (g b)"),
+                in_=hid.pop((e, hb))[:])
+
+        def epilogue(e, db):
+            banks = accs.pop(("u", e, db))
+            for j in range(W // NB):
+                cols = slice(db * W + j * NB, db * W + (j + 1) * NB)
+                if e == 0:
+                    m = mix.tile([B, NB], F32)
+                    nc.vector.scalar_tensor_tensor(
+                        out=m[:], in0=banks[j][:], scalar=gates["p"][:, 0:1], in1=bias_sb[:, cols], op0=ALU.mult, op1=ALU.add)
+                    mixed[(db, j)] = m
+                else:
+                    m2 = mix.tile([B, NB], F32)
+                    nc.vector.scalar_tensor_tensor(
+                        out=m2[:], in0=banks[j][:], scalar=gates["p"][:, 1:2], in1=mixed.pop((db, j))[:], op0=ALU.mult, op1=ALU.add)
+                    mixed[(db, j)] = m2
+            if e == 1:
+                prods = []
+                for j in range(W // NB):
+                    cols = slice(db * W + j * NB, db * W + (j + 1) * NB)
+                    m3 = mix.tile([B, NB], F32)
+                    nc.vector.tensor_tensor(out=m3[:], in0=mixed.pop((db, j))[:], in1=x0_sb[:, cols], op=ALU.mult)
+                    prods.append(m3)
+                for j in range(W // NB):
+                    cols = slice(db * W + j * NB, db * W + (j + 1) * NB)
+                    m4 = mix.tile([B, NB], F32)
+                    nc.vector.tensor_tensor(out=m4[:], in0=prods[j][:], in1=x_sb[:, cols], op=ALU.add)
+                    eng = nc.sync if db == DB - 1 else nc.scalar
+                    eng.dma_start(out=out[:, cols], in_=m4[:])
+
+        def softmax_gates():
+            top = small.tile([B, 1], F32)
+            nc.vector.tensor_reduce(out=top[:], in_=gate_sb[:], op=ALU.max, axis=AX.X)
+            shifted = small.tile([B, E], F32)
+            nc.vector.tensor_scalar(out=shifted[:], in0=gate_sb[:], scalar1=top[:], scalar2=None, op0=ALU.subtract)
+            ex = small.tile([B, E], F32)
+            nc.scalar.activation(out=ex[:], in_=shifted[:], func=ACT.Exp)
+            total = small.tile([B, 1], F32)
+            nc.vector.tensor_reduce(out=total[:], in_=ex[:], op=ALU.add, axis=AX.X)
+            inv = small.tile([B, 1], F32)
+            nc.vector.reciprocal(out=inv[:], in_=total[:])
+            p = const.tile([B, E], F32)
+            nc.vector.tensor_scalar(out=p[:], in0=ex[:], scalar1=inv[:], scalar2=None, op0=ALU.mult)
+            gates["p"] = p
+
+        make_identity(nc, ident[:])
+        with tc.manual_schedule():
+            nc.sync.dma_start(out=scale_sb[:], in_=v_scale.rearrange("o (g p t) u -> p (o g) (t u)", p=P, t=PACK))
+            load(0)
+            nc.sync.dma_start(out=x_sb[:], in_=x)
+            for i in range(1, 4):
+                load(i)
+            nc.sync.dma_start(out=gate_sb[:], in_=gate_logits)
+            loaded = [4, n_v]
+
+            for i in range(2):
+                widen(i)
+            x_groups = []
+            for q in range(3):
+                slots = tr_pool.tile([P, 4, B], F32)
+                turn(x_sb[:].bitcast(F32), q, slots)
+                xg = const.tile([P, 2 * B * PACK], BF16, align_bytes=64, name="xg%d" % q)
+                group_words(xg[:], slots[:])
+                x_groups.append(xg)
+            for q in range(3):
+                gs = slice(2 * q, 2 * q + 2)
+                nc.vector.quantize_mx(
+                    out=x_codes[:, gs, :].rearrange("p g b -> p (g b)").bitcast(FP8X4),
+                    scales=x_scales[:, gs, :].rearrange("p g b -> p (g b)"),
+                    in_=x_groups[q][:])
+            arrange(0)
+
+            later = {}
+
+            def at(step, fn, *args):
+                later.setdefault(step, []).append((fn, args))
+
+            for s in range(n + 4):
+                if s == 1:
+                    nc.sync.dma_start(out=c_sb[:], in_=c.rearrange("e r -> (e r)").partition_broadcast(P))
+                if s == 4:
+                    nc.sync.dma_start(out=bias_sb[:], in_=bias.partition_broadcast(P))
+                    nc.sync.dma_start(out=x0_sb[:], in_=x0)
+                while loaded[0] < min(n_v, s + 6):
+                    load(loaded[0])
+                    loaded[0] += 1
+                if s >= 6 and loaded[1] < n and (s < n_v - 2 and s % 2 == 0 and loaded[1] < n_v + 8 or loaded[1] < s + 8):
+                    load(loaded[1])
+                    loaded[1] += 1
+                if s + 2 < n:
+                    widen(s + 2)
+                if s + 1 < n:
+                    arrange(s + 1)
+                if s < n:
+                    quantize(s)
+                if s == 3:
+                    softmax_gates()
+                for fn, args in later.pop(s, []):
+                    fn(*args)
+                if s < n:
+                    multiply(s)
+                    kind, e, blk, g = units[s]
+                    if kind == "v" and g == V_PASSES - 1:
+                        at(s + 1, hidden_tanh, e, blk)
+                        at(s + 2, hidden_scale, e, blk)
+                        at(s + 3, hidden_group, e, blk)
+                        at(s + 4, hidden_quantize, e, blk)
+                    if kind == "u" and g == U_PASSES - 1:
+                        at(s + 1 if s < n - 1 else s + 1, epilogue, e, blk)

@@ -25,8 +25,10 @@ V_PASSES = D // K_PASS
 U_PASSES = R // K_PASS
 RH = R // W
 DB = D // W
-V_WIDEN = 352
-U_VEC = 448
+V_WIDEN = 320
+U_VEC = 432
+U_VEC_PE = 352
+U_PE = 256
 
 
 def tile_dcnv2lowrankexpertcross_w_kernel(tc, x0, x, v_bytes, v_scale, c, u, bias, gate_logits, out):
@@ -44,6 +46,7 @@ def tile_dcnv2lowrankexpertcross_w_kernel(tc, x0, x, v_bytes, v_scale, c, u, bia
         tr_pool = ctx.enter_context(tc.psum_pool(name="tr_pool", bufs=4))
 
         ident = const.tile([P, P], F32)
+        ident16 = const.tile([P, P], BF16)
         scale_sb = const.tile([P, V_PASSES, PACK], F32)
         x_sb = const.tile([B, D], BF16)
         x0_sb = const.tile([B, D], BF16)
@@ -67,6 +70,7 @@ def tile_dcnv2lowrankexpertcross_w_kernel(tc, x0, x, v_bytes, v_scale, c, u, bia
         hid = {}
         mixed = {}
         gates = {}
+        pe_out = {}
 
         def load(i):
             kind, e, blk, g = units[i]
@@ -87,15 +91,16 @@ def tile_dcnv2lowrankexpertcross_w_kernel(tc, x0, x, v_bytes, v_scale, c, u, bia
                 return
             v_wide = wide_pool.tile([P, PACK, W], BF16)
             v_raw = raw.pop(i)
-            cut = W - V_WIDEN
-            nc.vector.tensor_scalar(
-                out=v_wide[:, 3, cut:], in0=v_raw[:, 3, cut:].bitcast(FP8),
-                scalar1=scale_sb[:, g, 3:4], scalar2=None, op0=ALU.mult)
+            ends = {0: (W, W, 0, 0), 1: (W, W, W, 0)}.get(i, (W, W, W, W - V_WIDEN))
             for t in range(PACK):
-                end = W if t < 3 else cut
-                nc.scalar.activation(
-                    out=v_wide[:, t, :end], in_=v_raw[:, t, :end].bitcast(FP8),
-                    func=ACT.Copy, scale=scale_sb[:, g, t:t + 1])
+                if ends[t] < W:
+                    nc.vector.tensor_scalar(
+                        out=v_wide[:, t, ends[t]:], in0=v_raw[:, t, ends[t]:].bitcast(FP8),
+                        scalar1=scale_sb[:, g, t:t + 1], scalar2=None, op0=ALU.mult)
+                if ends[t] > 0:
+                    nc.scalar.activation(
+                        out=v_wide[:, t, :ends[t]], in_=v_raw[:, t, :ends[t]].bitcast(FP8),
+                        func=ACT.Copy, scale=scale_sb[:, g, t:t + 1])
             wide[i] = v_wide
 
         def interleave(copy, dst, src):
@@ -108,9 +113,25 @@ def tile_dcnv2lowrankexpertcross_w_kernel(tc, x0, x, v_bytes, v_scale, c, u, bia
                 interleave(nc.vector.tensor_copy, grouped[:], wide.pop(i)[:])
             else:
                 u_raw = raw.pop(i)
-                interleave(nc.vector.tensor_copy, grouped[:, :U_VEC, :], u_raw[:, :, :U_VEC])
-                interleave(nc.scalar.copy, grouped[:, U_VEC:, :], u_raw[:, :, U_VEC:])
+                on_pe = pe_out.pop(i, None)
+                a = U_VEC if on_pe is None else U_VEC_PE
+                b = W if on_pe is None else W - U_PE
+                interleave(nc.vector.tensor_copy, grouped[:, :a, :], u_raw[:, :, :a])
+                if on_pe is not None:
+                    nc.scalar.copy(out=grouped[:, b:, :].rearrange("p w t -> p (w t)"), in_=on_pe[:])
+                interleave(nc.scalar.copy, grouped[:, a:b, :], u_raw[:, :, a:b])
             inter[i] = grouped
+
+        def pe_interleave(i):
+            if units[i][0] == "v" or (i - n_v) % 5 == 0:
+                return
+            slots = tr_pool.tile([P, U_PE * PACK], BF16)
+            for j in range(U_PE // P):
+                cs = slice(W - U_PE + j * P, W - U_PE + (j + 1) * P)
+                nc.tensor.matmul(
+                    out=slots[:, j * NB:(j + 1) * NB], lhsT=ident16[:],
+                    rhs=raw[i][:, :, cs].rearrange("p t w -> p w t"), start=True, stop=True)
+            pe_out[i] = slots
 
         def quantize(i):
             w_codes = code_pool.tile([P, W], U32, align_bytes=64)
@@ -201,8 +222,7 @@ def tile_dcnv2lowrankexpertcross_w_kernel(tc, x0, x, v_bytes, v_scale, c, u, bia
                     cols = slice(db * W + j * NB, db * W + (j + 1) * NB)
                     m4 = mix.tile([B, NB], F32)
                     nc.vector.tensor_tensor(out=m4[:], in0=prods[j][:], in1=x_sb[:, cols], op=ALU.add)
-                    eng = nc.sync if db == DB - 1 else nc.scalar
-                    eng.dma_start(out=out[:, cols], in_=m4[:])
+                    nc.sync.dma_start(out=out[:, cols], in_=m4[:])
 
         def softmax_gates():
             top = small.tile([B, 1], F32)
@@ -220,6 +240,7 @@ def tile_dcnv2lowrankexpertcross_w_kernel(tc, x0, x, v_bytes, v_scale, c, u, bia
             gates["p"] = p
 
         make_identity(nc, ident[:])
+        nc.vector.tensor_copy(out=ident16[:], in_=ident[:])
         with tc.manual_schedule():
             nc.sync.dma_start(out=scale_sb[:], in_=v_scale.rearrange("o (g p t) u -> p (o g) (t u)", p=P, t=PACK))
             load(0)
@@ -265,6 +286,7 @@ def tile_dcnv2lowrankexpertcross_w_kernel(tc, x0, x, v_bytes, v_scale, c, u, bia
                     loaded[1] += 1
                 if s + 2 < n:
                     widen(s + 2)
+                    pe_interleave(s + 2)
                 if s + 1 < n:
                     arrange(s + 1)
                 if s < n:

from contextlib import ExitStack

import concourse.mybir as mybir
from concourse.masks import make_identity

B, D, R, E = 128, 3072, 2048, 2
P = 128
PACK = 4
K_PASS = P * PACK
FLOPS = 2 * 2 * E * B * D * R

F32 = mybir.dt.float32
BF16 = mybir.dt.bfloat16
U32 = mybir.dt.uint32
U8 = mybir.dt.uint8
FP8 = mybir.dt.float8_e4m3fn
FP8X4 = mybir.dt.float8_e4m3fn_x4
ACT = mybir.ActivationFunctionType
ALU = mybir.AluOpType
AX = mybir.AxisListType

W = 1024
NB = 512
V_PASSES = D // K_PASS
U_PASSES = R // K_PASS
RH = R // W
DB = D // W
V_WIDEN = 320
U_VEC = 432
U_VEC_PE = 352
U_PE = 256


def tile_dcnv2lowrankexpertcross_w_kernel(tc, x0, x, v_bytes, v_scale, c, u, bias, gate_logits, out):
    nc = tc.nc
    with ExitStack() as ctx:
        const = ctx.enter_context(tc.tile_pool(name="const", bufs=1))
        byte_pool = ctx.enter_context(tc.tile_pool(name="byte_pool", bufs=6))
        wide_pool = ctx.enter_context(tc.tile_pool(name="wide_pool", bufs=3))
        raw_pool = ctx.enter_context(tc.tile_pool(name="raw_pool", bufs=8))
        inter_pool = ctx.enter_context(tc.tile_pool(name="inter_pool", bufs=3))
        code_pool = ctx.enter_context(tc.tile_pool(name="code_pool", bufs=4))
        small = ctx.enter_context(tc.tile_pool(name="small", bufs=2))
        mix = ctx.enter_context(tc.tile_pool(name="mix", bufs=2))
        acc_pool = ctx.enter_context(tc.psum_pool(name="acc_pool", bufs=4))
        tr_pool = ctx.enter_context(tc.psum_pool(name="tr_pool", bufs=4))

        ident = const.tile([P, P], F32)
        ident16 = const.tile([P, P], BF16)
        scale_sb = const.tile([P, V_PASSES, PACK], F32)
        x_sb = const.tile([B, D], BF16)
        x0_sb = const.tile([B, D], BF16)
        bias_sb = const.tile([B, D], BF16)
        c_sb = const.tile([B, E, R], BF16)
        gate_sb = const.tile([B, E], BF16)
        x_codes = const.tile([P, V_PASSES, B], U32, align_bytes=64)
        x_scales = const.tile([P, V_PASSES, B], U8, align_bytes=64)
        h_codes = const.tile([P, E, U_PASSES, B], U32, align_bytes=64)
        h_scales = const.tile([P, E, U_PASSES, B], U8, align_bytes=64)

        units = [("v", e, hb, g) for e in range(E) for hb in range(RH) for g in range(V_PASSES)]
        n_v = len(units)
        units += [("u", e, db, g) for db in range(DB) for e in range(E) for g in range(U_PASSES)]
        n = len(units)
        raw = {}
        wide = {}
        inter = {}
        codes = {}
        accs = {}
        hid = {}
        mixed = {}
        gates = {}
        pe_out = {}

        def load(i):
            kind, e, blk, g = units[i]
            ks = slice(g * K_PASS, (g + 1) * K_PASS)
            cs = slice(blk * W, (blk + 1) * W)
            if kind == "v":
                v_raw = byte_pool.tile([P, PACK, W], U8)
                nc.sync.dma_start(out=v_raw[:], in_=v_bytes[e, ks, cs].rearrange("(p t) w -> p t w", t=PACK))
                raw[i] = v_raw
            else:
                u_raw = raw_pool.tile([P, PACK, W], BF16)
                nc.sync.dma_start(out=u_raw[:], in_=u[e, ks, cs].rearrange("(p t) w -> p t w", t=PACK))
                raw[i] = u_raw

        def widen(i):
            kind, e, blk, g = units[i]
            if kind == "u":
                return
            v_wide = wide_pool.tile([P, PACK, W], BF16)
            v_raw = raw.pop(i)
            ends = {0: (W, W, 0, 0), 1: (W, W, W, 0)}.get(i, (W, W, W, W - V_WIDEN))
            for t in range(PACK):
                if ends[t] < W:
                    nc.vector.tensor_scalar(
                        out=v_wide[:, t, ends[t]:], in0=v_raw[:, t, ends[t]:].bitcast(FP8),
                        scalar1=scale_sb[:, g, t:t + 1], scalar2=None, op0=ALU.mult)
                if ends[t] > 0:
                    nc.scalar.activation(
                        out=v_wide[:, t, :ends[t]], in_=v_raw[:, t, :ends[t]].bitcast(FP8),
                        func=ACT.Copy, scale=scale_sb[:, g, t:t + 1])
            wide[i] = v_wide

        def interleave(copy, dst, src):
            copy(out=dst.rearrange("p (c i) t -> p c t i", i=4), in_=src.rearrange("p t (c i) -> p c t i", i=4))

        def arrange(i):
            kind, e, blk, g = units[i]
            grouped = inter_pool.tile([P, W, PACK], BF16, align_bytes=64)
            if kind == "v":
                interleave(nc.vector.tensor_copy, grouped[:], wide.pop(i)[:])
            else:
                u_raw = raw.pop(i)
                on_pe = pe_out.pop(i, None)
                a = U_VEC if on_pe is None else U_VEC_PE
                b = W if on_pe is None else W - U_PE
                interleave(nc.vector.tensor_copy, grouped[:, :a, :], u_raw[:, :, :a])
                if on_pe is not None:
                    nc.scalar.copy(out=grouped[:, b:, :].rearrange("p w t -> p (w t)"), in_=on_pe[:])
                interleave(nc.scalar.copy, grouped[:, a:b, :], u_raw[:, :, a:b])
            inter[i] = grouped

        def pe_interleave(i):
            if units[i][0] == "v" or (i - n_v) % 5 == 0:
                return
            slots = tr_pool.tile([P, U_PE * PACK], BF16)
            for j in range(U_PE // P):
                cs = slice(W - U_PE + j * P, W - U_PE + (j + 1) * P)
                nc.tensor.matmul(
                    out=slots[:, j * NB:(j + 1) * NB], lhsT=ident16[:],
                    rhs=raw[i][:, :, cs].rearrange("p t w -> p w t"), start=True, stop=True)
            pe_out[i] = slots

        def quantize(i):
            w_codes = code_pool.tile([P, W], U32, align_bytes=64)
            w_scales = code_pool.tile([P, W], U8, align_bytes=64)
            nc.vector.quantize_mx(
                out=w_codes[:].bitcast(FP8X4), scales=w_scales[:],
                in_=inter.pop(i)[:].rearrange("p w t -> p (w t)"))
            codes[i] = (w_codes, w_scales)

        def multiply(i):
            kind, e, blk, g = units[i]
            w_codes, w_scales = codes.pop(i)
            last = (V_PASSES if kind == "v" else U_PASSES) - 1
            if g == 0:
                banks = []
                for j in range(W // NB):
                    acc = acc_pool.tile([B, NB], F32)
                    banks.append(acc)
                accs[(kind, e, blk)] = banks
            banks = accs[(kind, e, blk)]
            for j in range(W // NB):
                js = slice(j * NB, (j + 1) * NB)
                lhs = x_codes[:, g, :] if kind == "v" else h_codes[:, e, g, :]
                lhs_scale = x_scales[:, g, :] if kind == "v" else h_scales[:, e, g, :]
                nc.tensor.matmul_mx(
                    out=banks[j][:], lhsT=lhs.bitcast(FP8X4), lhsT_scale=lhs_scale,
                    rhs=w_codes[:, js].bitcast(FP8X4), rhs_scale=w_scales[:, js],
                    start=(g == 0), stop=(g == last))

        def turn(src_words, q, slots):
            for j in range(2):
                for w in range(2):
                    first = 256 * (2 * q + j)
                    nc.tensor.transpose(slots[:, 2 * j + w, :], src_words[:, first + w:first + 256:2], ident[:])

        def group_words(dst, slots):
            nc.vector.tensor_copy(
                out=dst.bitcast(F32).rearrange("p (j r w) -> p j r w", j=2, w=2),
                in_=slots.rearrange("p (j w) r -> p j r w", w=2))

        def hidden_tanh(e, hb):
            th = small.tile([B, W], F32)
            for j, acc in enumerate(accs.pop(("v", e, hb))):
                nc.scalar.activation(out=th[:, j * NB:(j + 1) * NB], in_=acc[:], func=ACT.Tanh)
            hid[(e, hb)] = th

        def hidden_scale(e, hb):
            h = small.tile([B, W], BF16)
            nc.vector.tensor_tensor(out=h[:], in0=hid[(e, hb)][:], in1=c_sb[:, e, hb * W:(hb + 1) * W], op=ALU.mult)
            slots = tr_pool.tile([P, 4, B], F32)
            turn(h[:].bitcast(F32), 0, slots)
            hid[(e, hb)] = slots

        def hidden_group(e, hb):
            hg = small.tile([P, 2 * B * PACK], BF16, align_bytes=64)
            group_words(hg[:], hid[(e, hb)][:])
            hid[(e, hb)] = hg

        def hidden_quantize(e, hb):
            gs = slice(2 * hb, 2 * hb + 2)
            nc.vector.quantize_mx(
                out=h_codes[:, e, gs, :].rearrange("p g b -> p (g b)").bitcast(FP8X4),
                scales=h_scales[:, e, gs, :].rearrange("p g b -> p (g b)"),
                in_=hid.pop((e, hb))[:])

        def epilogue(e, db):
            banks = accs.pop(("u", e, db))
            for j in range(W // NB):
                cols = slice(db * W + j * NB, db * W + (j + 1) * NB)
                if e == 0:
                    m = mix.tile([B, NB], F32)
                    nc.vector.scalar_tensor_tensor(
                        out=m[:], in0=banks[j][:], scalar=gates["p"][:, 0:1], in1=bias_sb[:, cols], op0=ALU.mult, op1=ALU.add)
                    mixed[(db, j)] = m
                else:
                    m2 = mix.tile([B, NB], F32)
                    nc.vector.scalar_tensor_tensor(
                        out=m2[:], in0=banks[j][:], scalar=gates["p"][:, 1:2], in1=mixed.pop((db, j))[:], op0=ALU.mult, op1=ALU.add)
                    mixed[(db, j)] = m2
            if e == 1:
                prods = []
                for j in range(W // NB):
                    cols = slice(db * W + j * NB, db * W + (j + 1) * NB)
                    m3 = mix.tile([B, NB], F32)
                    nc.vector.tensor_tensor(out=m3[:], in0=mixed.pop((db, j))[:], in1=x0_sb[:, cols], op=ALU.mult)
                    prods.append(m3)
                for j in range(W // NB):
                    cols = slice(db * W + j * NB, db * W + (j + 1) * NB)
                    m4 = mix.tile([B, NB], F32)
                    nc.vector.tensor_tensor(out=m4[:], in0=prods[j][:], in1=x_sb[:, cols], op=ALU.add)
                    nc.sync.dma_start(out=out[:, cols], in_=m4[:])

        def softmax_gates():
            top = small.tile([B, 1], F32)
            nc.vector.tensor_reduce(out=top[:], in_=gate_sb[:], op=ALU.max, axis=AX.X)
            shifted = small.tile([B, E], F32)
            nc.vector.tensor_scalar(out=shifted[:], in0=gate_sb[:], scalar1=top[:], scalar2=None, op0=ALU.subtract)
            ex = small.tile([B, E], F32)
            nc.scalar.activation(out=ex[:], in_=shifted[:], func=ACT.Exp)
            total = small.tile([B, 1], F32)
            nc.vector.tensor_reduce(out=total[:], in_=ex[:], op=ALU.add, axis=AX.X)
            inv = small.tile([B, 1], F32)
            nc.vector.reciprocal(out=inv[:], in_=total[:])
            p = const.tile([B, E], F32)
            nc.vector.tensor_scalar(out=p[:], in0=ex[:], scalar1=inv[:], scalar2=None, op0=ALU.mult)
            gates["p"] = p

        make_identity(nc, ident[:])
        nc.vector.tensor_copy(out=ident16[:], in_=ident[:])
        with tc.manual_schedule():
            nc.sync.dma_start(out=scale_sb[:], in_=v_scale.rearrange("o (g p t) u -> p (o g) (t u)", p=P, t=PACK))
            load(0)
            nc.sync.dma_start(out=x_sb[:], in_=x)
            for i in range(1, 4):
                load(i)
            nc.sync.dma_start(out=gate_sb[:], in_=gate_logits)
            loaded = [4, n_v]

            for i in range(2):
                widen(i)
            x_groups = []
            for q in range(3):
                slots = tr_pool.tile([P, 4, B], F32)
                turn(x_sb[:].bitcast(F32), q, slots)
                xg = const.tile([P, 2 * B * PACK], BF16, align_bytes=64, name="xg%d" % q)
                group_words(xg[:], slots[:])
                x_groups.append(xg)
            for q in range(3):
                gs = slice(2 * q, 2 * q + 2)
                nc.vector.quantize_mx(
                    out=x_codes[:, gs, :].rearrange("p g b -> p (g b)").bitcast(FP8X4),
                    scales=x_scales[:, gs, :].rearrange("p g b -> p (g b)"),
                    in_=x_groups[q][:])
            arrange(0)

            later = {}

            def at(step, fn, *args):
                later.setdefault(step, []).append((fn, args))

            for s in range(n + 4):
                if s == 1:
                    nc.sync.dma_start(out=c_sb[:], in_=c.rearrange("e r -> (e r)").partition_broadcast(P))
                if s == 4:
                    nc.sync.dma_start(out=bias_sb[:], in_=bias.partition_broadcast(P))
                    nc.sync.dma_start(out=x0_sb[:], in_=x0)
                while loaded[0] < min(n_v, s + 6):
                    load(loaded[0])
                    loaded[0] += 1
                if s >= 6 and loaded[1] < n and (s < n_v - 2 and s % 2 == 0 and loaded[1] < n_v + 8 or loaded[1] < s + 8):
                    load(loaded[1])
                    loaded[1] += 1
                if s + 2 < n:
                    widen(s + 2)
                    pe_interleave(s + 2)
                if s + 1 < n:
                    arrange(s + 1)
                if s < n:
                    quantize(s)
                if s == 3:
                    softmax_gates()
                for fn, args in later.pop(s, []):
                    fn(*args)
                if s < n:
                    multiply(s)
                    kind, e, blk, g = units[s]
                    if kind == "v" and g == V_PASSES - 1:
                        at(s + 1, hidden_tanh, e, blk)
                        at(s + 2, hidden_scale, e, blk)
                        at(s + 3, hidden_group, e, blk)
                        at(s + 4, hidden_quantize, e, blk)
                    if kind == "u" and g == U_PASSES - 1:
                        at(s + 1 if s < n - 1 else s + 1, epilogue, e, blk)
